import numpy as np
import ml_dtypes


def mxq(x, axis, fmt="e4m3"):
    dtype, down = {"e4m3": (ml_dtypes.float8_e4m3fn, 7), "e5m2": (ml_dtypes.float8_e5m2, 14)}[fmt]
    v = np.moveaxis(np.asarray(x, np.float32).astype(ml_dtypes.bfloat16).astype(np.float64), axis, -1)
    blocks = v.reshape(v.shape[:-1] + (-1, 32))
    amax = np.abs(blocks).max(-1, keepdims=True)
    byte = np.maximum(np.where(amax > 0, np.frexp(amax)[1] - 1 + 127, 0) - down, 1)
    scale = np.exp2(byte - 127.0)
    codes = (blocks / scale).astype(np.float32).astype(dtype).astype(np.float64)
    return np.moveaxis((codes * scale).reshape(v.shape), -1, axis)


WIDE = False


def mx_kscale(k):
    if not WIDE:
        return np.ones(k)
    levels = np.array([10, -10, 5, -5, 0])
    if k % 512:
        return np.exp2(np.random.permutation(np.resize(levels, k // 32))).repeat(32)
    a = np.empty((k // 512, 16))
    for p in range(k // 512):
        a[p, :8] = np.random.permutation(np.resize(levels, 8))
        for g in range(8):
            far = levels[np.abs(levels - a[p, g]) >= 10]
            a[p, g + 8] = far[np.random.randint(len(far))]
    return np.exp2(a.ravel()).repeat(32)


def f64(x):
    return np.asarray(x).astype(np.float64)


def striped(idx):
    return np.tile(idx.reshape(-1, 16).T, (8, 1)).astype(np.uint16)


def unstriped(offs):
    return offs[:16].T.reshape(-1).astype(np.int64)


def relu(v):
    return np.maximum(v, 0.0)


K, T, E, C, H, N = 2048, 512, 6, 256, 512, 128
TOP = 3


def by_expert(wq, xq):
    return np.concatenate([wq[e].T @ xq[:, e * C:(e + 1) * C] for e in range(E)], axis=1)


def setup_inputs():
    n = np.random.standard_normal
    s = mx_kscale(K)[:, None]
    u = mx_kscale(H)
    deal = np.repeat(np.arange(E), C).reshape(TOP, T)[:, np.random.permutation(T)]
    deal = np.take_along_axis(deal, np.argsort(np.random.rand(TOP, T), axis=0), axis=0)
    for _ in range(8):
        s_, t_ = np.random.permutation(T).reshape(2, -1); r = np.random.randint(TOP, size=T // 2); x, y = deal[r, s_].copy(), deal[r, t_].copy()
        ok = ~((deal[:, s_] == y).any(0) | (deal[:, t_] == x).any(0)); deal[r[ok], s_[ok]] = y[ok]; deal[r[ok], t_[ok]] = x[ok]
    order = np.lexsort((np.random.rand(TOP * T), deal.reshape(-1)))
    slot_token = order % T; pos = np.empty(TOP * T, np.int64); pos[order] = np.arange(TOP * T); pos = pos.reshape(TOP, T)
    g = np.random.uniform(0.5, 1.5, (TOP, T)); g = g / g.sum(0)
    return {
        "xT": (n((K, T)) * s).astype(np.float32),
        "w1": (n((E, K, H)) / np.sqrt(K) / s[None] * u[None, None, :]).astype(np.float32),
        "w2": (n((E, H, N)) / np.sqrt(H) / u[None, :, None]).astype(np.float32),
        "gate": np.stack([np.tile(r, (N, 1)) for r in g]).astype(np.float32),
        "offs": striped(slot_token),
        "pos1": striped(pos[0]),
        "pos2": striped(pos[1]),
        "pos3": striped(pos[2]),
    }


def reference(xT, w1, w2, gate, offs, pos1, pos2, pos3):
    idx = unstriped(offs)
    xq = mxq(f64(xT)[:, idx], 0, "e4m3")
    h = relu(by_expert(mxq(f64(w1), 1, "e4m3"), xq))
    y = by_expert(mxq(f64(w2), 1, "e4m3"), mxq(h, 0, "e4m3"))
    return sum(f64(gate[r]) * y[:, unstriped(p)] for r, p in enumerate((pos1, pos2, pos3)))

@@ -1,0 +1,183 @@
+from contextlib import ExitStack
+
+import concourse.mybir as mybir
+
+K, T, E, C, H, N, TOP = 2048, 512, 6, 256, 512, 128, 3
+
+FLOPS = 2 * TOP * T * (K * H + H * N)
+
+F32 = mybir.dt.float32
+BF16 = mybir.dt.bfloat16
+U32 = mybir.dt.uint32
+U16 = mybir.dt.uint16
+U8 = mybir.dt.uint8
+FP8X4 = mybir.dt.float8_e4m3fn_x4
+COPY = mybir.ActivationFunctionType.Copy
+RELU = mybir.ActivationFunctionType.Relu
+ADD = mybir.AluOpType.add
+MULT = mybir.AluOpType.mult
+
+P = 128
+J = 4
+S = K // (P * J)
+HT = H // P
+M = H // HT
+LIST = C // 16
+SPLIT = 4
+VECTOR_SHARE = (80, 64, 32, 0)
+LAST_SHARE = (80, 64, 64, 64)
+
+
+def tile_moe_tk_mlp_relu_kernel(tc, xT, w1, w2, gate, offs, pos1, pos2, pos3, out):
+    nc = tc.nc
+    with ExitStack() as ctx:
+        keep = ctx.enter_context(tc.tile_pool(name="keep", bufs=1))
+        stage = ctx.enter_context(tc.tile_pool(name="stage", bufs=12))
+        groups = ctx.enter_context(tc.tile_pool(name="groups", bufs=4))
+        work = ctx.enter_context(tc.tile_pool(name="work", bufs=3))
+        codes = ctx.enter_context(tc.tile_pool(name="codes", bufs=8))
+        psum = ctx.enter_context(tc.psum_pool(name="psum", bufs=8))
+
+        offsets = keep.tile([P, TOP * T // 16], U16, name="offsets")
+        nc.sync.dma_start(offsets[:], offs)
+
+        x_scales = keep.tile([P, T], U8, name="x_scales", align_bytes=64)
+        nc.gpsimd.memset(x_scales[:], 0)
+        x_words = []
+        for s in range(S):
+            raw = stage.tile([P, J, T], F32, name="raw", tag="raw", align_bytes=64)
+            nc.sync.dma_start(out=raw[:], in_=xT[s * P * J : (s + 1) * P * J, :].rearrange("(p j) t -> p j t", j=J))
+            grouped = groups.tile([P, T, J], BF16, name="xg", tag="grouped", align_bytes=64)
+            nc.scalar.activation(
+                grouped[:].rearrange("p (c i) j -> p c j i", i=4), raw[:].rearrange("p j (c i) -> p c j i", i=4), COPY
+            )
+            words = keep.tile([P, T], U32, name=f"x_words{s}", align_bytes=64)
+            nc.vector.quantize_mx(
+                out=words[:].bitcast(FP8X4),
+                scales=x_scales[4 * s :, :],
+                in_=grouped[:].rearrange("p t j -> p (t j)"),
+            )
+            x_words.append(words)
+
+        places = []
+        for r, pos in enumerate((pos1, pos2, pos3)):
+            place = keep.tile([P, T // 16], U16, name=f"place{r}")
+            nc.sync.dma_start(place[:], pos)
+            places.append(place)
+
+        w2_words = keep.tile([P, E, N], U32, name="w2_words", align_bytes=64)
+        w2_scales = keep.tile([P, E, N], U8, name="w2_scales", align_bytes=64)
+        y = keep.tile([P, E * C], F32, name="y", align_bytes=64)
+
+        def gather(e):
+            words = work.tile([P, S, C], U32, name="slot_words", align_bytes=64)
+            scales = work.tile([P, C], U8, name="slot_scales", align_bytes=64)
+            where = offsets[:, e * LIST : (e + 1) * LIST]
+            for s in range(S):
+                nc.vector.tensor_copy(words[:, s, :], x_words[s][:].indirect(where))
+            nc.vector.tensor_copy(scales[:], x_scales[:].indirect(where))
+            return words, scales
+
+        def chunk(e, s):
+            raw = stage.tile([P, J, H], F32, name="raw", tag="raw", align_bytes=64)
+            nc.sync.dma_start(out=raw[:], in_=w1[e, s * P * J : (s + 1) * P * J, :].rearrange("(p j) i -> p j i", j=J))
+            grouped = groups.tile([P, H, J], BF16, name="wg", tag="grouped", align_bytes=64)
+            src = raw[:].rearrange("p j (m t) -> p m j t", t=HT)
+            dst = grouped[:].rearrange("p (t m) j -> p m j t", t=HT)
+            cut = (LAST_SHARE if e == E - 1 else VECTOR_SHARE)[s]
+            if cut > 0:
+                nc.vector.tensor_copy(out=dst[:, :cut], in_=src[:, :cut])
+            nc.scalar.activation(dst[:, cut:], src[:, cut:], COPY)
+            words = codes.tile([P, H], U32, name="w1_words", align_bytes=64)
+            scales = codes.tile([P, H], U8, name="w1_scales", align_bytes=64)
+            nc.vector.quantize_mx(
+                out=words[:].bitcast(FP8X4), scales=scales[:], in_=grouped[:].rearrange("p h j -> p (h j)")
+            )
+            return words, scales
+
+        def second_weights(e0, e1, on_vector):
+            raw = stage.tile([P, e1 - e0, J * N], F32, name="raw", tag="raw", align_bytes=64)
+            nc.sync.dma_start(out=raw[:], in_=w2[e0:e1].rearrange("e (p j) n -> p e (j n)", j=J))
+            grouped = groups.tile([P, e1 - e0, N, J], BF16, name="w2g", tag="grouped", align_bytes=64)
+            src = raw[:].rearrange("p e (j n) -> p e n j", j=J)
+            if on_vector:
+                nc.vector.tensor_copy(out=grouped[:], in_=src)
+            else:
+                nc.scalar.activation(grouped[:], src, COPY)
+            nc.vector.quantize_mx(
+                out=w2_words[:, e0:e1, :].rearrange("p e n -> p (e n)").bitcast(FP8X4),
+                scales=w2_scales[:, e0:e1, :].rearrange("p e n -> p (e n)"),
+                in_=grouped[:].rearrange("p e n j -> p (e n j)"),
+            )
+
+        def second(e, h, engine_copy):
+            acc = psum.tile([P, C], F32, name="y_acc", tag="bank")
+            nc.tensor.matmul_mx(
+                out=acc[:],
+                lhsT=w2_words[:, e, :].bitcast(FP8X4),
+                lhsT_scale=w2_scales[:, e, :],
+                rhs=h[0][:].bitcast(FP8X4),
+                rhs_scale=h[1][:],
+                start=True,
+                stop=True,
+            )
+            engine_copy(y[:, e * C : (e + 1) * C], acc[:])
+
+        hidden = []
+        slots = gather(0)
+        for e in range(E):
+            banks = []
+            for t in range(HT):
+                bank = psum.tile([P, C], F32, name="h_acc", tag="bank")
+                banks.append(bank)
+            for s in range(S):
+                words, scales = chunk(e, s)
+                if s == 0 and e < E - 1:
+                    next_slots = gather(e + 1)
+                for t in range(HT):
+                    nc.tensor.matmul_mx(
+                        out=banks[t][:],
+                        lhsT=words[:, t * M : (t + 1) * M].bitcast(FP8X4),
+                        lhsT_scale=scales[:, t * M : (t + 1) * M],
+                        rhs=slots[0][:, s, :].bitcast(FP8X4),
+                        rhs_scale=slots[1][4 * s :, :],
+                        start=(s == 0),
+                        stop=(s == S - 1),
+                    )
+            if e == E - 1:
+                second_weights(0, SPLIT, True)
+                second_weights(SPLIT, E, False)
+                for d in range(E - 1):
+                    second(d, hidden[d], nc.scalar.copy)
+                gates = stage.tile([P, TOP, T], F32, name="raw", tag="raw", align_bytes=64)
+                nc.sync.dma_start(out=gates[:], in_=gate.rearrange("r n t -> n r t"))
+            h_rows = work.tile([P, HT, C], BF16, name="h_rows", align_bytes=64)
+            for t in range(HT):
+                if e == E - 1 and t < 2:
+                    nc.scalar.activation(h_rows[:, t, :], banks[t][:], RELU)
+                else:
+                    nc.vector.tensor_scalar_max(h_rows[:, t, :], banks[t][:], 0.0)
+            h_grouped = work.tile([P, C, HT], BF16, name="h_grouped", align_bytes=64)
+            nc.vector.tensor_copy(
+                out=h_grouped[:].rearrange("p (c i) t -> p c t i", i=4),
+                in_=h_rows[:].rearrange("p t (c i) -> p c t i", i=4),
+            )
+            h_words = codes.tile([P, C], U32, name="h_words", align_bytes=64)
+            h_scales = codes.tile([P, C], U8, name="h_scales", align_bytes=64)
+            nc.vector.quantize_mx(
+                out=h_words[:].bitcast(FP8X4), scales=h_scales[:], in_=h_grouped[:].rearrange("p c t -> p (c t)")
+            )
+            hidden.append((h_words, h_scales))
+            slots = next_slots
+        second(E - 1, hidden[E - 1], nc.vector.tensor_copy)
+
+        products = []
+        for r in range(TOP):
+            product = keep.tile([P, T], F32, name=f"product{r}", align_bytes=64)
+            nc.vector.tensor_tensor(product[:], y[:].indirect(places[r][:]), gates[:, r, :], MULT)
+            products.append(product)
+        pair = keep.tile([P, T], F32, name="pair", align_bytes=64)
+        nc.vector.tensor_tensor(pair[:], products[0][:], products[1][:], ADD)
+        total = keep.tile([P, T], F32, name="total", align_bytes=64)
+        nc.vector.tensor_tensor(total[:], pair[:], products[2][:], ADD)
+        nc.sync.dma_start(out=out, in_=total[:])

@@ -24,8 +24,8 @@ HT = H // P
 M = H // HT
 LIST = C // 16
 SPLIT = 4
-VECTOR_SHARE = (80, 64, 32, 0)
-LAST_SHARE = (80, 64, 64, 64)
+VECTOR_SHARE = (64, 0, 0, 0)
+LAST_SHARE = (64, 0, 64, 72)
 
 
 def tile_moe_tk_mlp_relu_kernel(tc, xT, w1, w2, gate, offs, pos1, pos2, pos3, out):
@@ -153,7 +153,7 @@ def tile_moe_tk_mlp_relu_kernel(tc, xT, w1, w2, gate, offs, pos1, pos2, pos3, ou
                 nc.sync.dma_start(out=gates[:], in_=gate.rearrange("r n t -> n r t"))
             h_rows = work.tile([P, HT, C], BF16, name="h_rows", align_bytes=64)
             for t in range(HT):
-                if e == E - 1 and t < 2:
+                if e == E - 1 and t % 2 == 0:
                     nc.scalar.activation(h_rows[:, t, :], banks[t][:], RELU)
                 else:
                     nc.vector.tensor_scalar_max(h_rows[:, t, :], banks[t][:], 0.0)

@@ -23,33 +23,40 @@ S = K // (P * J)
 HT = H // P
 M = H // HT
 LIST = C // 16
-SPLIT = 4
-VECTOR_SHARE = (64, 0, 0, 0)
-LAST_SHARE = (64, 0, 64, 72)
+VECTOR_SHARE = (48, 96, 32, 0)
+LAST_SHARE = (128, 48, 0, 72)
+REPEATS = (0, 4, 5, 0)
 
 
 def tile_moe_tk_mlp_relu_kernel(tc, xT, w1, w2, gate, offs, pos1, pos2, pos3, out):
     nc = tc.nc
     with ExitStack() as ctx:
         keep = ctx.enter_context(tc.tile_pool(name="keep", bufs=1))
-        stage = ctx.enter_context(tc.tile_pool(name="stage", bufs=12))
+        stage = ctx.enter_context(tc.tile_pool(name="stage", bufs=7))
         groups = ctx.enter_context(tc.tile_pool(name="groups", bufs=4))
         work = ctx.enter_context(tc.tile_pool(name="work", bufs=3))
         codes = ctx.enter_context(tc.tile_pool(name="codes", bufs=8))
         psum = ctx.enter_context(tc.psum_pool(name="psum", bufs=8))
 
-        offsets = keep.tile([P, TOP * T // 16], U16, name="offsets")
-        nc.sync.dma_start(offsets[:], offs)
+        def load(rows, passes):
+            raw = stage.tile([P, passes, J, rows.shape[1]], F32, name="raw", tag="raw", align_bytes=64)
+            nc.sync.dma_start(
+                out=raw[:].rearrange("p s j c -> p s (j c)"),
+                in_=rows.rearrange("(s p j) c -> p s (j c)", s=passes, j=J),
+            )
+            return [raw[:, s, :, :] for s in range(passes)]
 
         x_scales = keep.tile([P, T], U8, name="x_scales", align_bytes=64)
         nc.gpsimd.memset(x_scales[:], 0)
+        offsets = keep.tile([P, TOP * T // 16], U16, name="offsets")
+        x_raw = load(xT[0 : P * J, :], 1) + load(xT[P * J : 2 * P * J, :], 1)
+        nc.sync.dma_start(offsets[:], offs)
+        x_raw = x_raw + load(xT[2 * P * J :, :], 2)
         x_words = []
         for s in range(S):
-            raw = stage.tile([P, J, T], F32, name="raw", tag="raw", align_bytes=64)
-            nc.sync.dma_start(out=raw[:], in_=xT[s * P * J : (s + 1) * P * J, :].rearrange("(p j) t -> p j t", j=J))
             grouped = groups.tile([P, T, J], BF16, name="xg", tag="grouped", align_bytes=64)
             nc.scalar.activation(
-                grouped[:].rearrange("p (c i) j -> p c j i", i=4), raw[:].rearrange("p j (c i) -> p c j i", i=4), COPY
+                grouped[:].rearrange("p (c i) j -> p c j i", i=4), x_raw[s].rearrange("p j (c i) -> p c j i", i=4), COPY
             )
             words = keep.tile([P, T], U32, name=f"x_words{s}", align_bytes=64)
             nc.vector.quantize_mx(
@@ -58,12 +65,6 @@ def tile_moe_tk_mlp_relu_kernel(tc, xT, w1, w2, gate, offs, pos1, pos2, pos3, ou
                 in_=grouped[:].rearrange("p t j -> p (t j)"),
             )
             x_words.append(words)
-
-        places = []
-        for r, pos in enumerate((pos1, pos2, pos3)):
-            place = keep.tile([P, T // 16], U16, name=f"place{r}")
-            nc.sync.dma_start(place[:], pos)
-            places.append(place)
 
         w2_words = keep.tile([P, E, N], U32, name="w2_words", align_bytes=64)
         w2_scales = keep.tile([P, E, N], U8, name="w2_scales", align_bytes=64)
@@ -78,21 +79,22 @@ def tile_moe_tk_mlp_relu_kernel(tc, xT, w1, w2, gate, offs, pos1, pos2, pos3, ou
             nc.vector.tensor_copy(scales[:], x_scales[:].indirect(where))
             return words, scales
 
-        def chunk(e, s):
-            raw = stage.tile([P, J, H], F32, name="raw", tag="raw", align_bytes=64)
-            nc.sync.dma_start(out=raw[:], in_=w1[e, s * P * J : (s + 1) * P * J, :].rearrange("(p j) i -> p j i", j=J))
+        def chunk(raw, cut, step):
             grouped = groups.tile([P, H, J], BF16, name="wg", tag="grouped", align_bytes=64)
-            src = raw[:].rearrange("p j (m t) -> p m j t", t=HT)
+            src = raw.rearrange("p j (m t) -> p m j t", t=HT)
             dst = grouped[:].rearrange("p (t m) j -> p m j t", t=HT)
-            cut = (LAST_SHARE if e == E - 1 else VECTOR_SHARE)[s]
             if cut > 0:
                 nc.vector.tensor_copy(out=dst[:, :cut], in_=src[:, :cut])
-            nc.scalar.activation(dst[:, cut:], src[:, cut:], COPY)
+            if cut < M:
+                nc.scalar.activation(dst[:, cut:], src[:, cut:], COPY)
             words = codes.tile([P, H], U32, name="w1_words", align_bytes=64)
             scales = codes.tile([P, H], U8, name="w1_scales", align_bytes=64)
-            nc.vector.quantize_mx(
-                out=words[:].bitcast(FP8X4), scales=scales[:], in_=grouped[:].rearrange("p h j -> p (h j)")
-            )
+            for lo in range(0, H, step):
+                nc.vector.quantize_mx(
+                    out=words[:, lo : lo + step].bitcast(FP8X4),
+                    scales=scales[:, lo : lo + step],
+                    in_=grouped[:, lo : lo + step, :].rearrange("p h j -> p (h j)"),
+                )
             return words, scales
 
         def second_weights(e0, e1, on_vector):
@@ -110,74 +112,108 @@ def tile_moe_tk_mlp_relu_kernel(tc, xT, w1, w2, gate, offs, pos1, pos2, pos3, ou
                 in_=grouped[:].rearrange("p e n j -> p (e n j)"),
             )
 
-        def second(e, h, engine_copy):
+        def second(e, lo, hi):
             acc = psum.tile([P, C], F32, name="y_acc", tag="bank")
+            words, scales = hidden[e]
             nc.tensor.matmul_mx(
-                out=acc[:],
+                out=acc[:, : hi - lo],
                 lhsT=w2_words[:, e, :].bitcast(FP8X4),
                 lhsT_scale=w2_scales[:, e, :],
-                rhs=h[0][:].bitcast(FP8X4),
-                rhs_scale=h[1][:],
+                rhs=words[:, lo:hi].bitcast(FP8X4),
+                rhs_scale=scales[:, lo:hi],
                 start=True,
                 stop=True,
             )
-            engine_copy(y[:, e * C : (e + 1) * C], acc[:])
+            nc.scalar.copy(y[:, e * C + lo : e * C + hi], acc[:, : hi - lo])
 
         hidden = []
         slots = gather(0)
         for e in range(E):
+            last = e == E - 1
             banks = []
             for t in range(HT):
                 bank = psum.tile([P, C], F32, name="h_acc", tag="bank")
                 banks.append(bank)
             for s in range(S):
-                words, scales = chunk(e, s)
-                if s == 0 and e < E - 1:
+                row = s * P * J
+                if last and s >= 2:
+                    raws = load(w1[e, row : row + P * J, :], 1)
+                elif s % 2 == 0:
+                    raws = load(w1[e, row : row + 2 * P * J, :], 2)
+                words, scales = chunk(
+                    raws[s % len(raws)], (LAST_SHARE if last else VECTOR_SHARE)[s], M if last and s == S - 1 else H
+                )
+                if s == 1 and not last:
                     next_slots = gather(e + 1)
-                for t in range(HT):
+
+                def product(acc, t, start, stop):
                     nc.tensor.matmul_mx(
-                        out=banks[t][:],
+                        out=acc,
                         lhsT=words[:, t * M : (t + 1) * M].bitcast(FP8X4),
                         lhsT_scale=scales[:, t * M : (t + 1) * M],
                         rhs=slots[0][:, s, :].bitcast(FP8X4),
                         rhs_scale=slots[1][4 * s :, :],
-                        start=(s == 0),
-                        stop=(s == S - 1),
+                        start=start,
+                        stop=stop,
                     )
-            if e == E - 1:
-                second_weights(0, SPLIT, True)
-                second_weights(SPLIT, E, False)
+
+                for t in range(HT):
+                    product(banks[t][:], t, s == 0, s == S - 1)
+                if last and REPEATS[s] > 0:
+                    spare = psum.tile([P, C], F32, name="spare", tag="bank")
+                    for r in range(REPEATS[s]):
+                        product(spare[:], r % HT, True, True)
+            if last:
+                second_weights(0, 2, True)
+                second_weights(2, 4, False)
+                second_weights(4, 6, True)
                 for d in range(E - 1):
-                    second(d, hidden[d], nc.scalar.copy)
+                    second(d, 0, C)
+                places = []
+                for r, pos in enumerate((pos1, pos2, pos3)):
+                    place = keep.tile([P, T // 16], U16, name=f"place{r}")
+                    nc.sync.dma_start(place[:], pos)
+                    places.append(place)
                 gates = stage.tile([P, TOP, T], F32, name="raw", tag="raw", align_bytes=64)
-                nc.sync.dma_start(out=gates[:], in_=gate.rearrange("r n t -> n r t"))
+                for r in range(TOP):
+                    nc.sync.dma_start(out=gates[:, r, :], in_=gate[r])
             h_rows = work.tile([P, HT, C], BF16, name="h_rows", align_bytes=64)
             for t in range(HT):
-                if e == E - 1 and t % 2 == 0:
-                    nc.scalar.activation(h_rows[:, t, :], banks[t][:], RELU)
-                else:
+                if last and t % 2 == 1:
                     nc.vector.tensor_scalar_max(h_rows[:, t, :], banks[t][:], 0.0)
+                else:
+                    nc.scalar.activation(h_rows[:, t, :], banks[t][:], RELU)
             h_grouped = work.tile([P, C, HT], BF16, name="h_grouped", align_bytes=64)
-            nc.vector.tensor_copy(
-                out=h_grouped[:].rearrange("p (c i) t -> p c t i", i=4),
-                in_=h_rows[:].rearrange("p t (c i) -> p c t i", i=4),
-            )
             h_words = codes.tile([P, C], U32, name="h_words", align_bytes=64)
             h_scales = codes.tile([P, C], U8, name="h_scales", align_bytes=64)
-            nc.vector.quantize_mx(
-                out=h_words[:].bitcast(FP8X4), scales=h_scales[:], in_=h_grouped[:].rearrange("p c t -> p (c t)")
-            )
             hidden.append((h_words, h_scales))
+            parts = [(0, C // 2), (C // 2, C)] if last else [(0, C)]
+            for lo, hi in parts:
+                nc.vector.tensor_copy(
+                    out=h_grouped[:, lo:hi, :].rearrange("p (c i) t -> p c t i", i=4),
+                    in_=h_rows[:, :, lo:hi].rearrange("p t (c i) -> p c t i", i=4),
+                )
+            for lo, hi in parts:
+                nc.vector.quantize_mx(
+                    out=h_words[:, lo:hi].bitcast(FP8X4),
+                    scales=h_scales[:, lo:hi],
+                    in_=h_grouped[:, lo:hi, :].rearrange("p c t -> p (c t)"),
+                )
+            if last:
+                for lo, hi in parts:
+                    second(e, lo, hi)
             slots = next_slots
-        second(E - 1, hidden[E - 1], nc.vector.tensor_copy)
 
         products = []
         for r in range(TOP):
-            product = keep.tile([P, T], F32, name=f"product{r}", align_bytes=64)
-            nc.vector.tensor_tensor(product[:], y[:].indirect(places[r][:]), gates[:, r, :], MULT)
-            products.append(product)
+            scaled = keep.tile([P, T], F32, name=f"scaled{r}", align_bytes=64)
+            nc.vector.tensor_tensor(scaled[:], y[:].indirect(places[r][:]), gates[:, r, :], MULT)
+            products.append(scaled)
         pair = keep.tile([P, T], F32, name="pair", align_bytes=64)
-        nc.vector.tensor_tensor(pair[:], products[0][:], products[1][:], ADD)
         total = keep.tile([P, T], F32, name="total", align_bytes=64)
-        nc.vector.tensor_tensor(total[:], pair[:], products[2][:], ADD)
-        nc.sync.dma_start(out=out, in_=total[:])
+        halves = [slice(0, T // 2), slice(T // 2, T)]
+        for cols in halves:
+            nc.vector.tensor_tensor(pair[:, cols], products[0][:, cols], products[1][:, cols], ADD)
+        for cols in halves:
+            nc.vector.tensor_tensor(total[:, cols], pair[:, cols], products[2][:, cols], ADD)
+            nc.sync.dma_start(out=out[:, cols], in_=total[:, cols])

@@ -23,40 +23,37 @@ S = K // (P * J)
 HT = H // P
 M = H // HT
 LIST = C // 16
-VECTOR_SHARE = (48, 96, 32, 0)
-LAST_SHARE = (128, 48, 0, 72)
-REPEATS = (0, 4, 5, 0)
+VECTOR_SHARE = (0, 16, 64, 0)
+LAST_SHARE = (64, 32, 48, 88)
+REPEATS = (0, 0, 0, 0)
 
 
 def tile_moe_tk_mlp_relu_kernel(tc, xT, w1, w2, gate, offs, pos1, pos2, pos3, out):
     nc = tc.nc
     with ExitStack() as ctx:
         keep = ctx.enter_context(tc.tile_pool(name="keep", bufs=1))
-        stage = ctx.enter_context(tc.tile_pool(name="stage", bufs=7))
+        stage = ctx.enter_context(tc.tile_pool(name="stage", bufs=12))
         groups = ctx.enter_context(tc.tile_pool(name="groups", bufs=4))
         work = ctx.enter_context(tc.tile_pool(name="work", bufs=3))
         codes = ctx.enter_context(tc.tile_pool(name="codes", bufs=8))
         psum = ctx.enter_context(tc.psum_pool(name="psum", bufs=8))
 
-        def load(rows, passes):
-            raw = stage.tile([P, passes, J, rows.shape[1]], F32, name="raw", tag="raw", align_bytes=64)
-            nc.sync.dma_start(
-                out=raw[:].rearrange("p s j c -> p s (j c)"),
-                in_=rows.rearrange("(s p j) c -> p s (j c)", s=passes, j=J),
-            )
-            return [raw[:, s, :, :] for s in range(passes)]
+        def load(rows):
+            raw = stage.tile([P, J, rows.shape[1]], F32, name="raw", tag="raw", align_bytes=64)
+            nc.sync.dma_start(out=raw[:], in_=rows.rearrange("(p j) c -> p j c", j=J))
+            return raw[:]
 
         x_scales = keep.tile([P, T], U8, name="x_scales", align_bytes=64)
         nc.gpsimd.memset(x_scales[:], 0)
         offsets = keep.tile([P, TOP * T // 16], U16, name="offsets")
-        x_raw = load(xT[0 : P * J, :], 1) + load(xT[P * J : 2 * P * J, :], 1)
-        nc.sync.dma_start(offsets[:], offs)
-        x_raw = x_raw + load(xT[2 * P * J :, :], 2)
         x_words = []
         for s in range(S):
+            if s == S // 2:
+                nc.sync.dma_start(offsets[:], offs)
+            raw = load(xT[s * P * J : (s + 1) * P * J, :])
             grouped = groups.tile([P, T, J], BF16, name="xg", tag="grouped", align_bytes=64)
             nc.scalar.activation(
-                grouped[:].rearrange("p (c i) j -> p c j i", i=4), x_raw[s].rearrange("p j (c i) -> p c j i", i=4), COPY
+                grouped[:].rearrange("p (c i) j -> p c j i", i=4), raw.rearrange("p j (c i) -> p c j i", i=4), COPY
             )
             words = keep.tile([P, T], U32, name=f"x_words{s}", align_bytes=64)
             nc.vector.quantize_mx(
@@ -112,7 +109,7 @@ def tile_moe_tk_mlp_relu_kernel(tc, xT, w1, w2, gate, offs, pos1, pos2, pos3, ou
                 in_=grouped[:].rearrange("p e n j -> p (e n j)"),
             )
 
-        def second(e, lo, hi):
+        def second(e, lo, hi, copy_out):
             acc = psum.tile([P, C], F32, name="y_acc", tag="bank")
             words, scales = hidden[e]
             nc.tensor.matmul_mx(
@@ -124,7 +121,7 @@ def tile_moe_tk_mlp_relu_kernel(tc, xT, w1, w2, gate, offs, pos1, pos2, pos3, ou
                 start=True,
                 stop=True,
             )
-            nc.scalar.copy(y[:, e * C + lo : e * C + hi], acc[:, : hi - lo])
+            copy_out(y[:, e * C + lo : e * C + hi], acc[:, : hi - lo])
 
         hidden = []
         slots = gather(0)
@@ -135,15 +132,10 @@ def tile_moe_tk_mlp_relu_kernel(tc, xT, w1, w2, gate, offs, pos1, pos2, pos3, ou
                 bank = psum.tile([P, C], F32, name="h_acc", tag="bank")
                 banks.append(bank)
             for s in range(S):
-                row = s * P * J
-                if last and s >= 2:
-                    raws = load(w1[e, row : row + P * J, :], 1)
-                elif s % 2 == 0:
-                    raws = load(w1[e, row : row + 2 * P * J, :], 2)
                 words, scales = chunk(
-                    raws[s % len(raws)], (LAST_SHARE if last else VECTOR_SHARE)[s], M if last and s == S - 1 else H
+                    load(w1[e, s * P * J : (s + 1) * P * J, :]), (LAST_SHARE if last else VECTOR_SHARE)[s], M if last and s == S - 1 else H
                 )
-                if s == 1 and not last:
+                if s == S - 1 and not last:
                     next_slots = gather(e + 1)
 
                 def product(acc, t, start, stop):
@@ -168,7 +160,7 @@ def tile_moe_tk_mlp_relu_kernel(tc, xT, w1, w2, gate, offs, pos1, pos2, pos3, ou
                 second_weights(2, 4, False)
                 second_weights(4, 6, True)
                 for d in range(E - 1):
-                    second(d, 0, C)
+                    second(d, 0, C, nc.scalar.copy)
                 places = []
                 for r, pos in enumerate((pos1, pos2, pos3)):
                     place = keep.tile([P, T // 16], U16, name=f"place{r}")
@@ -179,10 +171,10 @@ def tile_moe_tk_mlp_relu_kernel(tc, xT, w1, w2, gate, offs, pos1, pos2, pos3, ou
                     nc.sync.dma_start(out=gates[:, r, :], in_=gate[r])
             h_rows = work.tile([P, HT, C], BF16, name="h_rows", align_bytes=64)
             for t in range(HT):
-                if last and t % 2 == 1:
-                    nc.vector.tensor_scalar_max(h_rows[:, t, :], banks[t][:], 0.0)
-                else:
+                if last and t % 2 == 0:
                     nc.scalar.activation(h_rows[:, t, :], banks[t][:], RELU)
+                else:
+                    nc.vector.tensor_scalar_max(h_rows[:, t, :], banks[t][:], 0.0)
             h_grouped = work.tile([P, C, HT], BF16, name="h_grouped", align_bytes=64)
             h_words = codes.tile([P, C], U32, name="h_words", align_bytes=64)
             h_scales = codes.tile([P, C], U8, name="h_scales", align_bytes=64)
@@ -201,7 +193,7 @@ def tile_moe_tk_mlp_relu_kernel(tc, xT, w1, w2, gate, offs, pos1, pos2, pos3, ou
                 )
             if last:
                 for lo, hi in parts:
-                    second(e, lo, hi)
+                    second(e, lo, hi, nc.vector.tensor_copy)
             slots = next_slots
 
         products = []

from contextlib import ExitStack

import concourse.mybir as mybir

K, T, E, C, H, N, TOP = 2048, 512, 6, 256, 512, 128, 3

FLOPS = 2 * TOP * T * (K * H + H * N)

F32 = mybir.dt.float32
BF16 = mybir.dt.bfloat16
U32 = mybir.dt.uint32
U16 = mybir.dt.uint16
U8 = mybir.dt.uint8
FP8X4 = mybir.dt.float8_e4m3fn_x4
COPY = mybir.ActivationFunctionType.Copy
RELU = mybir.ActivationFunctionType.Relu
ADD = mybir.AluOpType.add
MULT = mybir.AluOpType.mult

P = 128
J = 4
S = K // (P * J)
HT = H // P
M = H // HT
LIST = C // 16
VECTOR_SHARE = (0, 16, 64, 0)
LAST_SHARE = (64, 32, 48, 88)
REPEATS = (0, 0, 0, 0)


def tile_moe_tk_mlp_relu_kernel(tc, xT, w1, w2, gate, offs, pos1, pos2, pos3, out):
    nc = tc.nc
    with ExitStack() as ctx:
        keep = ctx.enter_context(tc.tile_pool(name="keep", bufs=1))
        stage = ctx.enter_context(tc.tile_pool(name="stage", bufs=12))
        groups = ctx.enter_context(tc.tile_pool(name="groups", bufs=4))
        work = ctx.enter_context(tc.tile_pool(name="work", bufs=3))
        codes = ctx.enter_context(tc.tile_pool(name="codes", bufs=8))
        psum = ctx.enter_context(tc.psum_pool(name="psum", bufs=8))

        def load(rows):
            raw = stage.tile([P, J, rows.shape[1]], F32, name="raw", tag="raw", align_bytes=64)
            nc.sync.dma_start(out=raw[:], in_=rows.rearrange("(p j) c -> p j c", j=J))
            return raw[:]

        x_scales = keep.tile([P, T], U8, name="x_scales", align_bytes=64)
        nc.gpsimd.memset(x_scales[:], 0)
        offsets = keep.tile([P, TOP * T // 16], U16, name="offsets")
        x_words = []
        for s in range(S):
            if s == S // 2:
                nc.sync.dma_start(offsets[:], offs)
            raw = load(xT[s * P * J : (s + 1) * P * J, :])
            grouped = groups.tile([P, T, J], BF16, name="xg", tag="grouped", align_bytes=64)
            nc.scalar.activation(
                grouped[:].rearrange("p (c i) j -> p c j i", i=4), raw.rearrange("p j (c i) -> p c j i", i=4), COPY
            )
            words = keep.tile([P, T], U32, name=f"x_words{s}", align_bytes=64)
            nc.vector.quantize_mx(
                out=words[:].bitcast(FP8X4),
                scales=x_scales[4 * s :, :],
                in_=grouped[:].rearrange("p t j -> p (t j)"),
            )
            x_words.append(words)

        w2_words = keep.tile([P, E, N], U32, name="w2_words", align_bytes=64)
        w2_scales = keep.tile([P, E, N], U8, name="w2_scales", align_bytes=64)
        y = keep.tile([P, E * C], F32, name="y", align_bytes=64)

        def gather(e):
            words = work.tile([P, S, C], U32, name="slot_words", align_bytes=64)
            scales = work.tile([P, C], U8, name="slot_scales", align_bytes=64)
            where = offsets[:, e * LIST : (e + 1) * LIST]
            for s in range(S):
                nc.vector.tensor_copy(words[:, s, :], x_words[s][:].indirect(where))
            nc.vector.tensor_copy(scales[:], x_scales[:].indirect(where))
            return words, scales

        def chunk(raw, cut, step):
            grouped = groups.tile([P, H, J], BF16, name="wg", tag="grouped", align_bytes=64)
            src = raw.rearrange("p j (m t) -> p m j t", t=HT)
            dst = grouped[:].rearrange("p (t m) j -> p m j t", t=HT)
            if cut > 0:
                nc.vector.tensor_copy(out=dst[:, :cut], in_=src[:, :cut])
            if cut < M:
                nc.scalar.activation(dst[:, cut:], src[:, cut:], COPY)
            words = codes.tile([P, H], U32, name="w1_words", align_bytes=64)
            scales = codes.tile([P, H], U8, name="w1_scales", align_bytes=64)
            for lo in range(0, H, step):
                nc.vector.quantize_mx(
                    out=words[:, lo : lo + step].bitcast(FP8X4),
                    scales=scales[:, lo : lo + step],
                    in_=grouped[:, lo : lo + step, :].rearrange("p h j -> p (h j)"),
                )
            return words, scales

        def second_weights(e0, e1, on_vector):
            raw = stage.tile([P, e1 - e0, J * N], F32, name="raw", tag="raw", align_bytes=64)
            nc.sync.dma_start(out=raw[:], in_=w2[e0:e1].rearrange("e (p j) n -> p e (j n)", j=J))
            grouped = groups.tile([P, e1 - e0, N, J], BF16, name="w2g", tag="grouped", align_bytes=64)
            src = raw[:].rearrange("p e (j n) -> p e n j", j=J)
            if on_vector:
                nc.vector.tensor_copy(out=grouped[:], in_=src)
            else:
                nc.scalar.activation(grouped[:], src, COPY)
            nc.vector.quantize_mx(
                out=w2_words[:, e0:e1, :].rearrange("p e n -> p (e n)").bitcast(FP8X4),
                scales=w2_scales[:, e0:e1, :].rearrange("p e n -> p (e n)"),
                in_=grouped[:].rearrange("p e n j -> p (e n j)"),
            )

        def second(e, lo, hi, copy_out):
            acc = psum.tile([P, C], F32, name="y_acc", tag="bank")
            words, scales = hidden[e]
            nc.tensor.matmul_mx(
                out=acc[:, : hi - lo],
                lhsT=w2_words[:, e, :].bitcast(FP8X4),
                lhsT_scale=w2_scales[:, e, :],
                rhs=words[:, lo:hi].bitcast(FP8X4),
                rhs_scale=scales[:, lo:hi],
                start=True,
                stop=True,
            )
            copy_out(y[:, e * C + lo : e * C + hi], acc[:, : hi - lo])

        hidden = []
        slots = gather(0)
        for e in range(E):
            last = e == E - 1
            banks = []
            for t in range(HT):
                bank = psum.tile([P, C], F32, name="h_acc", tag="bank")
                banks.append(bank)
            for s in range(S):
                words, scales = chunk(
                    load(w1[e, s * P * J : (s + 1) * P * J, :]), (LAST_SHARE if last else VECTOR_SHARE)[s], M if last and s == S - 1 else H
                )
                if s == S - 1 and not last:
                    next_slots = gather(e + 1)

                def product(acc, t, start, stop):
                    nc.tensor.matmul_mx(
                        out=acc,
                        lhsT=words[:, t * M : (t + 1) * M].bitcast(FP8X4),
                        lhsT_scale=scales[:, t * M : (t + 1) * M],
                        rhs=slots[0][:, s, :].bitcast(FP8X4),
                        rhs_scale=slots[1][4 * s :, :],
                        start=start,
                        stop=stop,
                    )

                for t in range(HT):
                    product(banks[t][:], t, s == 0, s == S - 1)
                if last and REPEATS[s] > 0:
                    spare = psum.tile([P, C], F32, name="spare", tag="bank")
                    for r in range(REPEATS[s]):
                        product(spare[:], r % HT, True, True)
            if last:
                second_weights(0, 2, True)
                second_weights(2, 4, False)
                second_weights(4, 6, True)
                for d in range(E - 1):
                    second(d, 0, C, nc.scalar.copy)
                places = []
                for r, pos in enumerate((pos1, pos2, pos3)):
                    place = keep.tile([P, T // 16], U16, name=f"place{r}")
                    nc.sync.dma_start(place[:], pos)
                    places.append(place)
                gates = stage.tile([P, TOP, T], F32, name="raw", tag="raw", align_bytes=64)
                for r in range(TOP):
                    nc.sync.dma_start(out=gates[:, r, :], in_=gate[r])
            h_rows = work.tile([P, HT, C], BF16, name="h_rows", align_bytes=64)
            for t in range(HT):
                if last and t % 2 == 0:
                    nc.scalar.activation(h_rows[:, t, :], banks[t][:], RELU)
                else:
                    nc.vector.tensor_scalar_max(h_rows[:, t, :], banks[t][:], 0.0)
            h_grouped = work.tile([P, C, HT], BF16, name="h_grouped", align_bytes=64)
            h_words = codes.tile([P, C], U32, name="h_words", align_bytes=64)
            h_scales = codes.tile([P, C], U8, name="h_scales", align_bytes=64)
            hidden.append((h_words, h_scales))
            parts = [(0, C // 2), (C // 2, C)] if last else [(0, C)]
            for lo, hi in parts:
                nc.vector.tensor_copy(
                    out=h_grouped[:, lo:hi, :].rearrange("p (c i) t -> p c t i", i=4),
                    in_=h_rows[:, :, lo:hi].rearrange("p t (c i) -> p c t i", i=4),
                )
            for lo, hi in parts:
                nc.vector.quantize_mx(
                    out=h_words[:, lo:hi].bitcast(FP8X4),
                    scales=h_scales[:, lo:hi],
                    in_=h_grouped[:, lo:hi, :].rearrange("p c t -> p (c t)"),
                )
            if last:
                for lo, hi in parts:
                    second(e, lo, hi, nc.vector.tensor_copy)
            slots = next_slots

        products = []
        for r in range(TOP):
            scaled = keep.tile([P, T], F32, name=f"scaled{r}", align_bytes=64)
            nc.vector.tensor_tensor(scaled[:], y[:].indirect(places[r][:]), gates[:, r, :], MULT)
            products.append(scaled)
        pair = keep.tile([P, T], F32, name="pair", align_bytes=64)
        total = keep.tile([P, T], F32, name="total", align_bytes=64)
        halves = [slice(0, T // 2), slice(T // 2, T)]
        for cols in halves:
            nc.vector.tensor_tensor(pair[:, cols], products[0][:, cols], products[1][:, cols], ADD)
        for cols in halves:
            nc.vector.tensor_tensor(total[:, cols], pair[:, cols], products[2][:, cols], ADD)
            nc.sync.dma_start(out=out[:, cols], in_=total[:, cols])
